import numpy as np, ml_dtypes
CORES = [8,9,10,11,12,13]
N = 6
import mx_ref
BF = ml_dtypes.bfloat16
def entries(a):
    return np.ascontiguousarray(a.T).reshape(-1)
def table(e):
    return np.ascontiguousarray(np.reshape(e, (-1, 16)).T).astype(np.int32)
def cols(t, e):
    v = np.concatenate([t.reshape(128, -1, 4), np.zeros((128, 1, 4), BF)], axis=1)
    return np.ascontiguousarray(v[:, e]).reshape(128, -1)
def f(rng, *shape):
    return mx_ref.flush((rng.standard_normal(shape, dtype=np.float32) * np.exp2(rng.integers(-2, 3, shape[:-1] + (1,)))).astype(BF))
def wide(rng, *shape, cols=0):
    v = rng.standard_normal(shape, dtype=np.float32) * np.exp2(rng.integers(-12, 13, shape)).astype(np.float32)
    if cols: v *= np.repeat(np.exp2(rng.integers(-cols, cols + 1, shape[:-2] + (1, shape[-1] // 4))) * (rng.random(shape[:-2] + (1, shape[-1] // 4)) > 0.0625), 4, axis=-1).astype(np.float32)
    return mx_ref.flush(v.astype(BF))
B, K, O = 256, 96, 3
def order(r):
    return [(r + 1 + i) % N for i in range(N)]
def some(rng, where, n):
    e = np.full(K, -1); e[rng.permutation(K)[:n]] = rng.permutation(where)[:n]
    return table(e)
def setup_inputs(rng):
    return {"b": f(rng, N, 128, 4 * B), "x": f(rng, N, 128, 4 * K), "w": f(rng, N, 128, 512 * O), "pl": np.stack([some(rng, np.arange(B), int(rng.integers(K >> 1, K + 1))) for r in range(N)])}
def setup_inputs_same(rng):
    d = setup_inputs(rng)
    for i in range(50):
        at = rng.permutation(B)[:K]; quiet = rng.permutation(N)[:int(rng.integers(1, 3))].tolist()
        pl = [some(rng, at, 0 if r in quiet else int(rng.integers(K >> 2, (3 * K >> 2) + 1))) for r in range(N)]
        s = [set(entries(pl[r]).tolist()) - {-1} for r in range(N) if r not in quiet]
        if all(s[j] & s[k] for j in range(len(s)) for k in range(j)):
            d["pl"] = np.stack(pl); return d
    raise RuntimeError("no draw in which any two of the writing ranks have a place in common")
def setup_inputs_apart(rng):
    d = setup_inputs(rng); at, start = rng.permutation(B), int(rng.integers(N))
    pl = [None] * N
    for i in range(N):
        e = at[K * i:K * i + K]
        pl[(start + i) % N] = some(rng, e, len(e))
    d["pl"] = np.stack(pl); return d
def setup_inputs_runs(rng):
    d = setup_inputs(rng); p = rng.permutation(N)
    pl = [None] * N
    for i in range(N):
        if i == 0: at = np.arange(0)
        elif i % 3 == 1: at = (int(rng.integers(B)) + np.arange(K)) % B
        elif i % 3 == 2: at = np.flatnonzero(np.isin(np.arange(B) % 8, rng.permutation(8)[:8 * K // B]))
        else: at = rng.permutation(B)[:K - int(rng.integers(K >> 2, (3 * K >> 2) + 1))]
        at = rng.permutation(at); a = int(rng.integers(len(at) + 1))
        pl[p[i]] = table(np.concatenate([at[:a], np.full(K - len(at), -1), at[a:]]))
    d["pl"] = np.stack(pl); return d
def setup_inputs_halves(rng):
    d = setup_inputs(rng); at, start = rng.permutation(B), int(rng.integers(N))
    pl = [None] * N
    for i in range(N): pl[(start + i) % N] = some(rng, at[:B >> 1] if i < N >> 1 else at[B >> 1:], K)
    d["pl"] = np.stack(pl); return d
def setup_inputs_spread(rng):
    d = setup_inputs(rng); d["b"] = wide(rng, N, 128, 4 * B, cols=6); d["x"] = wide(rng, N, 128, 4 * K, cols=6); return d
def check_inputs(d):
    bad = []
    for r in range(N):
        e = entries(d["pl"][r])
        if e.min() < -1 or e.max() >= B: bad.append("pl")
        e = e[e >= 0]
        if len(set(e.tolist())) != len(e): bad.append("pl names a place twice")
    return bad
def reference(b, x, w, pl):
    y = np.zeros((N, 128, O * B), np.float32)
    for r in range(N):
        m = np.array(b[r]).reshape(128, B, 4)
        for s in order(r):
            e = entries(pl[s]); k = np.flatnonzero(e >= 0)
            m[:, e[k]] = x[s].reshape(128, K, 4)[:, k]
        q = mx_ref.quantize(m.reshape(128, 4 * B))
        for o in range(O):
            y[r][:, B * o:B * o + B] = mx_ref.matmul(mx_ref.quantize(cols(w[r], np.arange(128 * o, 128 * o + 128))), q)
    return {"y": y}

@@ -1,0 +1,206 @@
+from concourse.bass import DstId, RemoteDMATransfer
+from concourse.mybir import dt, AluOpType, ActivationFunctionType
+
+N, B, K, O = 6, 256, 96, 3
+OWN = B + K * (N - 1)
+WIDE = OWN + K
+ALL = OWN + 128
+DUM = B + 192
+NONE = -1024.0
+
+
+def slot(d):
+    return B + K * (N - 1 - d)
+
+
+SCRATCH = {
+    "xt": ("sbuf", [128, 512], "bfloat16"),
+    "bt": ("sbuf", [128, 4 * B], "bfloat16"),
+    "wt": ("sbuf", [128, 512 * O], "bfloat16"),
+    "q": ("sbuf", [128, ALL], "float8_e4m3fn_x4"),
+    "sq": ("sbuf", [128, ALL], "uint8"),
+    "wq": ("sbuf", [128, 128 * O], "float8_e4m3fn_x4"),
+    "wsq": ("sbuf", [128, 128 * O], "uint8"),
+    "m": ("sbuf", [128, B], "float8_e4m3fn_x4"),
+    "ms": ("sbuf", [128, B], "uint8"),
+    "ys": ("sbuf", [128, O * B], "float32"),
+    "ps": ("psum", [128, 3072], "float32"),
+    "own": ("sbuf", [128, 3], "int32"),
+    "nd": ("sbuf", [128, 3], "int32"),
+    "sh": ("sbuf", [128, 1], "float32"),
+    "u": ("sbuf", [128, 3], "int32"),
+    "vd": ("sbuf", [128, 3], "int32"),
+    "off": ("sbuf", [128, 4], "uint16"),
+    "val": ("sbuf", [128, 48], "float32"),
+    "win": ("sbuf", [128, DUM + 384], "float32"),
+    "tt": ("sbuf", [128, 64], "float32"),
+    "land": ("sbuf", [128, 8 * N], "bfloat16"),
+    "pf": ("sbuf", [128, 2], "float32"),
+    "ini": ("sbuf", [128, 2], "float32"),
+    "dl": ("sbuf", [128, N], "float32"),
+    "hm": ("sbuf", [128, 2], "float32"),
+    "sc": ("sbuf", [128, 2 * N], "float32"),
+    "in2": ("sbuf", [128, 32], "float32"),
+    "t2": ("sbuf", [128, 64], "float32"),
+    "mk": ("sbuf", [128, 16], "float32"),
+    "f2": ("sbuf", [128, 64], "float32"),
+    "pick": ("sbuf", [128, 16], "uint16"),
+}
+SEMAPHORES = ["sx", "sb", "sw", "sw2", "sp", "gi", "gn", "v", "qx", "qb", "qw0", "qw1", "qw2", "al", "ac", "asc", "loc",
+              "ofs", "shs", "cs", "ms0", "scn", "cp", "hms", "mks", "offr", "pkv0", "pkv1", "pks0", "pks1", "sy"]
+SEMAPHORES += ["mm%d" % i for i in range(6)] + ["c%d" % i for i in range(6)]
+
+
+def rank_program(g, core, T, topo):
+    r = T.rank_of(core)
+    if r is None:
+        return
+    A, s = AluOpType, T.sem
+    V, S, P, Y = g.vector, g.scalar, g.tensor, g.sync
+    Copy, Identity = ActivationFunctionType.Copy, ActivationFunctionType.Identity
+
+    for a, e in ((0, Y), (1, Y), (2, S), (3, S)):
+        e.dma_start(T.own[32 * a:32 * a + 32, :], T.pl[:]).then_inc(s.sp, 16)
+    Y.dma_start(T.xt[:, 0:4 * K], T.x[:]).then_inc(s.sx, 16)
+    Y.dma_start(T.bt[:], T.b[:]).then_inc(s.sb, 16)
+    Y.dma_start(T.wt[:, 0:512], T.w[:, 0:512]).then_inc(s.sw, 16)
+    Y.dma_start(T.wt[:, 512:1536], T.w[:, 512:1536]).then_inc(s.sw2, 16)
+
+    n = [0]
+
+    def v(ins):
+        n[0] += 1
+        return ins.then_inc(s.v, 1)
+
+    def vw():
+        V.wait_ge(s.v, n[0])
+
+    imprecise = {"allow_small_or_imprecise_dtypes": True}
+    g.iota(T.nd[:], [[-128, 3]], -DUM, -1).then_inc(s.gi, 1)
+    g.iota(T.val[:], [[16, 3], [1, 8], [48, 2]], -15, 1, **imprecise).then_inc(s.gi, 1)
+    g.iota(T.pf[:], [[32, 2]], -64, 1, **imprecise).then_inc(s.gn, 1)
+
+    others = [(r + 1 + i) % N for i in range(N - 1)]
+    ids, mask = [], None
+    for o in others:
+        rid, pid, _se = topo.addr(T.cores[o])
+        ids.append(DstId(rid=rid, pnc=pid))
+        k = topo.mask(core, T.cores[o])
+        mask = k if mask is None else mask & k
+    eng = len([e for e in topo.engines(core, T.cores[others[0]])])
+    ds = [(o - r) % N for o in others]
+
+    def send(src, dst, sem, a=0, b=N - 1):
+        g.remote_dma_fused([RemoteDMATransfer(dst_ids=ids[a:b], dma_engine_mask=mask, remote_sem=sem, srcs=[src],
+                                              dsts=[dst(d) for d in ds[a:b]])], local_sem=s.loc)
+
+    def scales(d):
+        return T.sq[:, slot(d):slot(d) + K]
+
+    me = 8 * (N - 1)
+    g.wait_ge(s.qx, 1)
+    send(T.sq[:, OWN:WIDE], scales, s.asc, 0, 1)
+    g.wait_ge(s.ofs, 1)
+    send(T.land[:, me:me + 2], lambda d: T.land[:, 8 * (N - 1 - d):8 * (N - 1 - d) + 2], s.al)
+    send(T.q[:, OWN:WIDE].bitcast(dt.uint8), lambda d: T.q[:, slot(d):slot(d) + K].bitcast(dt.uint8), s.ac)
+    send(T.sq[:, OWN:WIDE], scales, s.asc, 1)
+
+    for a in range(4):
+        V.memset(T.sh[32 * a:32 * a + 32, :], 192.0 - 64 * a).then_inc(s.shs, 1)
+    v(V.memset(T.win[:, 192:256], NONE))
+    v(V.memset(T.xt[:, 4 * K:512], 0.0))
+    vw()
+    V.wait_ge(s.shs, 4)
+    V.wait_ge(s.gi, 2)
+    V.wait_ge(s.sp, 64)
+    v(V.tensor_scalar(T.u[:], T.own[:], T.sh[:], None, A.add))
+    v(V.tensor_tensor(T.vd[:], T.own[:], T.nd[:], A.mult))
+    vw()
+    v(V.tensor_tensor(T.off[:, 0:3], T.u[:], T.vd[:], A.max))
+    V.wait_ge(s.sx, 16)
+    V.quantize_mx(T.q[:, OWN:ALL], T.sq[:, OWN:ALL], T.xt[:]).then_inc(s.qx, 1)
+    vw()
+    v(V.tensor_copy(T.win[:].indirect(T.off[:, 0:3]), T.val[:]))
+    vw()
+    v(V.transpose(T.tt[:], T.win[:, 192:256]))
+    vw()
+    V.tensor_tensor(T.land[:, me:me + 2], T.tt[:, 15:64:32], T.tt[:, 23:64:32], A.max).then_inc(s.ofs, 1)
+    V.memset(T.in2[0:32, :], 0.0).then_inc(s.ms0, 1)
+    V.memset(T.t2[0:32, :], 0.0).then_inc(s.ms0, 1)
+    V.memset(T.dl[:, 0:N - 1], float(-K)).then_inc(s.cs, 1)
+    V.wait_ge(s.gn, 1)
+    V.tensor_scalar(T.hm[0:32, 0:1], T.pf[0:32, 0:1], -48.0, None, A.is_lt).then_inc(s.hms, 1)
+    V.tensor_scalar(T.hm[0:32, 1:2], T.pf[0:32, 0:1], -48.0, None, A.is_ge).then_inc(s.hms, 1)
+    V.wait_ge(s.sb, 16)
+    V.quantize_mx(T.q[:, 0:B], T.sq[:, 0:B], T.bt[:]).then_inc(s.qb, 1)
+    for o in range(O):
+        if o < 2:
+            V.wait_ge(s.sw2 if o else s.sw, 16)
+        V.quantize_mx(T.wq[:, 128 * o:128 * o + 128], T.wsq[:, 128 * o:128 * o + 128],
+                      T.wt[:, 512 * o:512 * o + 512]).then_inc(s["qw%d" % o], 1)
+
+    S.wait_ge(s.shs, 4)
+    S.wait_ge(s.gn, 1)
+    S.activation(T.dl[:, N - 1:N], T.sh[:], Copy, bias=640.0, scale=0.5).then_inc(s.cs, 1)
+    for t in (0, 1):
+        S.activation(T.ini[:, t:t + 1], T.sh[:], Identity, bias=T.pf[:, t:t + 1], scale=-1.0).then_inc(s.cs, 1)
+    S.wait_ge(s.ms0, 2)
+    S.wait_ge(s.hms, 2)
+    S.wait_ge(s.qx, 1)
+    S.wait_ge(s.qb, 1)
+
+    V.wait_ge(s.cs, 4)
+    V.wait_ge(s.ms0, 2)
+    V.wait_ge(s.ofs, 1)
+    V.wait_ge(s.qx, 1)
+    V.wait_ge(s.qb, 1)
+    V.wait_ge(s.al, eng * (N - 1))
+    for t in (0, 1):
+        V.tensor_tensor_scan(T.sc[:, N * t:N * t + N], T.land[:, t:8 * N:8], T.dl[:], T.ini[:, t:t + 1], A.max, A.add).then_inc(s.scn, 1)
+    V.wait_ge(s.scn, 2)
+    S.wait_ge(s.scn, 2)
+    for a in range(4):
+        out, src = T.in2[0:32, 2 * a:2 * a + 2], T.sc[32 * a:32 * a + 32, N - 1:2 * N:N]
+        (V.tensor_copy(out, src) if a < 2 else S.activation(out, src, Copy)).then_inc(s.cp, 1)
+    V.wait_ge(s.cp, 4)
+    S.wait_ge(s.cp, 4)
+    v(V.transpose(T.t2[0:32, 16:48], T.in2[0:32, :]))
+    for h in (0, 1):
+        S.activation(T.mk[0:32, h:16:2], T.in2[0:32, 0:8], Identity, scale=T.hm[0:32, h:h + 1]).then_inc(s.mks, 1)
+    vw()
+    for h in (0, 1):
+        v(V.transpose(T.f2[0:32, h:64:2], T.t2[0:32, 32 * h:32 * h + 32]))
+    V.wait_ge(s.mks, 2)
+    vw()
+    for a in range(4):
+        V.tensor_tensor(T.pick[32 * a:32 * a + 32, :], T.f2[0:32, 0:16], T.mk[0:32, :], A.max).then_inc(s.offr, 1)
+
+    V.wait_ge(s.ac, eng * (N - 1))
+    V.wait_ge(s.offr, 4)
+    S.wait_ge(s.asc, eng * (N - 1))
+    S.wait_ge(s.offr, 4)
+    for h in (0, 1):
+        o = T.pick[:, 8 * h:8 * h + 8]
+        V.tensor_copy(T.m[:, 128 * h:128 * h + 128].bitcast(dt.uint32), T.q[:, 0:WIDE].bitcast(dt.uint32).indirect(o)).then_inc(s["pkv%d" % h], 1)
+        S.activation(T.ms[:, 128 * h:128 * h + 128], T.sq[:, 0:WIDE].indirect(o), Copy).then_inc(s["pks%d" % h], 1)
+
+    seq = [(h, o) for h in (0, 1) for o in range(O)]
+    for o in range(O):
+        P.wait_ge(s["qw%d" % o], 1)
+    for i, (h, o) in enumerate(seq):
+        if o == 0:
+            P.wait_ge(s["pkv%d" % h], 1)
+            P.wait_ge(s["pks%d" % h], 1)
+        P.matmul_mx(T.ps[:, 512 * i:512 * i + 128], T.wq[:, 128 * o:128 * o + 128], T.wsq[:, 128 * o:128 * o + 128],
+                    T.m[:, 128 * h:128 * h + 128], T.ms[:, 128 * h:128 * h + 128], True, True).then_inc(s["mm%d" % i], 1)
+    for i, (h, o) in enumerate(seq):
+        e = V if i in (0, 2, 4) else S
+        c = 256 * o + 128 * h
+        e.wait_ge(s["mm%d" % i], 1)
+        out, src = T.ys[:, c:c + 128], T.ps[:, 512 * i:512 * i + 128]
+        (V.tensor_copy(out, src) if e is V else S.activation(out, src, Copy)).then_inc(s["c%d" % i], 1)
+        Y.wait_ge(s["c%d" % i], 1)
+        Y.dma_start(T.y[:, c:c + 128], T.ys[:, c:c + 128]).then_inc(s.sy, 16)
+    Y.wait_ge(s.sy, 96)
+    V.wait_ge(s.v, n[0])
+    g.wait_ge(s.loc, 4 * eng)

@@ -2,10 +2,13 @@ from concourse.bass import DstId, RemoteDMATransfer
 from concourse.mybir import dt, AluOpType, ActivationFunctionType
 
 N, B, K, O = 6, 256, 96, 3
-OWN = B + K * (N - 1)
+HEAD = 16
+GAP = 128 - HEAD
+OWN = B + K * (N - 1) + GAP
 WIDE = OWN + K
-ALL = OWN + 128
-DUM = B + 192
+ALL = OWN + HEAD + 128
+STEP = 64
+SEEN = 97 * STEP
 NONE = -1024.0
 
 
@@ -14,7 +17,7 @@ def slot(d):
 
 
 SCRATCH = {
-    "xt": ("sbuf", [128, 512], "bfloat16"),
+    "xt": ("sbuf", [128, 1024], "bfloat16"),
     "bt": ("sbuf", [128, 4 * B], "bfloat16"),
     "wt": ("sbuf", [128, 512 * O], "bfloat16"),
     "q": ("sbuf", [128, ALL], "float8_e4m3fn_x4"),
@@ -26,28 +29,29 @@ SCRATCH = {
     "ys": ("sbuf", [128, O * B], "float32"),
     "ps": ("psum", [128, 3072], "float32"),
     "own": ("sbuf", [128, 3], "int32"),
-    "nd": ("sbuf", [128, 3], "int32"),
+    "nd": ("sbuf", [128, 3], "float32"),
+    "spare": ("sbuf", [128, 3], "float32"),
     "sh": ("sbuf", [128, 1], "float32"),
-    "u": ("sbuf", [128, 3], "int32"),
-    "vd": ("sbuf", [128, 3], "int32"),
+    "sh2": ("sbuf", [128, 1], "float32"),
+    "u": ("sbuf", [128, 3], "float32"),
     "off": ("sbuf", [128, 4], "uint16"),
-    "val": ("sbuf", [128, 48], "float32"),
-    "win": ("sbuf", [128, DUM + 384], "float32"),
-    "tt": ("sbuf", [128, 64], "float32"),
+    "val": ("sbuf", [128, 48], "bfloat16"),
+    "win": ("sbuf", [128, SEEN + STEP * B], "bfloat16"),
+    "tt": ("sbuf", [128, 64], "bfloat16"),
     "land": ("sbuf", [128, 8 * N], "bfloat16"),
     "pf": ("sbuf", [128, 2], "float32"),
     "ini": ("sbuf", [128, 2], "float32"),
     "dl": ("sbuf", [128, N], "float32"),
     "hm": ("sbuf", [128, 2], "float32"),
-    "sc": ("sbuf", [128, 2 * N], "float32"),
-    "in2": ("sbuf", [128, 32], "float32"),
+    "sc": ("sbuf", [128, 2 * N + 30], "float32"),
     "t2": ("sbuf", [128, 64], "float32"),
     "mk": ("sbuf", [128, 16], "float32"),
-    "f2": ("sbuf", [128, 64], "float32"),
+    "f2": ("sbuf", [128, 256], "float32"),
     "pick": ("sbuf", [128, 16], "uint16"),
 }
-SEMAPHORES = ["sx", "sb", "sw", "sw2", "sp", "gi", "gn", "v", "qx", "qb", "qw0", "qw1", "qw2", "al", "ac", "asc", "loc",
-              "ofs", "shs", "cs", "ms0", "scn", "cp", "hms", "mks", "offr", "pkv0", "pkv1", "pks0", "pks1", "sy"]
+SEMAPHORES = ["sx", "sx2", "sb", "sw", "sw2", "sp", "sp1", "sp2", "gd", "gi", "gn", "z0", "z1", "v", "qx", "qx2", "qb", "qw0", "qw1",
+              "qw2", "al", "ac", "asc", "loc", "ofs", "shs", "cs", "scn", "hms", "mks", "tb", "tab", "offr0", "offr1",
+              "pkv0", "pkv1", "pks0", "pks1", "sy"]
 SEMAPHORES += ["mm%d" % i for i in range(6)] + ["c%d" % i for i in range(6)]
 
 
@@ -59,9 +63,10 @@ def rank_program(g, core, T, topo):
     V, S, P, Y = g.vector, g.scalar, g.tensor, g.sync
     Copy, Identity = ActivationFunctionType.Copy, ActivationFunctionType.Identity
 
-    for a, e in ((0, Y), (1, Y), (2, S), (3, S)):
+    Y.dma_start(T.xt[:, 4 * GAP:512], T.x[:, 0:4 * HEAD]).then_inc(s.sx, 16)
+    for a, e in ((0, S), (1, Y)):
         e.dma_start(T.own[32 * a:32 * a + 32, :], T.pl[:]).then_inc(s.sp, 16)
-    Y.dma_start(T.xt[:, 0:4 * K], T.x[:]).then_inc(s.sx, 16)
+    Y.dma_start(T.xt[:, 512:4 * (GAP + K)], T.x[:, 4 * HEAD:4 * K]).then_inc(s.sx2, 16)
     Y.dma_start(T.bt[:], T.b[:]).then_inc(s.sb, 16)
     Y.dma_start(T.wt[:, 0:512], T.w[:, 0:512]).then_inc(s.sw, 16)
     Y.dma_start(T.wt[:, 512:1536], T.w[:, 512:1536]).then_inc(s.sw2, 16)
@@ -76,9 +81,9 @@ def rank_program(g, core, T, topo):
         V.wait_ge(s.v, n[0])
 
     imprecise = {"allow_small_or_imprecise_dtypes": True}
-    g.iota(T.nd[:], [[-128, 3]], -DUM, -1).then_inc(s.gi, 1)
+    g.iota(T.nd[:], [[16, 3]], 0, 1, **imprecise).then_inc(s.gd, 1)
     g.iota(T.val[:], [[16, 3], [1, 8], [48, 2]], -15, 1, **imprecise).then_inc(s.gi, 1)
-    g.iota(T.pf[:], [[32, 2]], -64, 1, **imprecise).then_inc(s.gn, 1)
+    g.iota(T.pf[:], [[128, 2]], -159, 1, **imprecise).then_inc(s.gn, 1)
 
     others = [(r + 1 + i) % N for i in range(N - 1)]
     ids, mask = [], None
@@ -90,8 +95,9 @@ def rank_program(g, core, T, topo):
     eng = len([e for e in topo.engines(core, T.cores[others[0]])])
     ds = [(o - r) % N for o in others]
 
-    def send(src, dst, sem, a=0, b=N - 1):
-        g.remote_dma_fused([RemoteDMATransfer(dst_ids=ids[a:b], dma_engine_mask=mask, remote_sem=sem, srcs=[src],
+    def send(src, dst, sem, a=0, b=N - 1, other=None):
+        g.remote_dma_fused([RemoteDMATransfer(dst_ids=ids[a:b], dma_engine_mask=mask, remote_sem=sem,
+                                              srcs=[src] if other is None else [src, other], alu_op=0 if other is None else 2,
                                               dsts=[dst(d) for d in ds[a:b]])], local_sem=s.loc)
 
     def scales(d):
@@ -99,38 +105,41 @@ def rank_program(g, core, T, topo):
 
     me = 8 * (N - 1)
     g.wait_ge(s.qx, 1)
-    send(T.sq[:, OWN:WIDE], scales, s.asc, 0, 1)
-    g.wait_ge(s.ofs, 1)
+    send(T.sq[:, OWN:OWN + HEAD], lambda d: T.sq[:, slot(d):slot(d) + HEAD], s.asc, 0, 1)
+    g.wait_ge(s.tab, 1)
     send(T.land[:, me:me + 2], lambda d: T.land[:, 8 * (N - 1 - d):8 * (N - 1 - d) + 2], s.al)
+    g.wait_ge(s.qx2, 1)
     send(T.q[:, OWN:WIDE].bitcast(dt.uint8), lambda d: T.q[:, slot(d):slot(d) + K].bitcast(dt.uint8), s.ac)
     send(T.sq[:, OWN:WIDE], scales, s.asc, 1)
+    send(T.sq[:, OWN + HEAD:WIDE], lambda d: T.sq[:, slot(d) + HEAD:slot(d) + K], s.asc, 0, 1)
 
+    V.memset(T.xt[:, 0:4 * GAP], 0.0).then_inc(s.z0, 1)
     for a in range(4):
-        V.memset(T.sh[32 * a:32 * a + 32, :], 192.0 - 64 * a).then_inc(s.shs, 1)
-    v(V.memset(T.win[:, 192:256], NONE))
-    v(V.memset(T.xt[:, 4 * K:512], 0.0))
-    vw()
-    V.wait_ge(s.shs, 4)
-    V.wait_ge(s.gi, 2)
-    V.wait_ge(s.sp, 64)
-    v(V.tensor_scalar(T.u[:], T.own[:], T.sh[:], None, A.add))
-    v(V.tensor_tensor(T.vd[:], T.own[:], T.nd[:], A.mult))
-    vw()
-    v(V.tensor_tensor(T.off[:, 0:3], T.u[:], T.vd[:], A.max))
+        V.memset(T.sh[32 * a:32 * a + 32, :], float(SEEN - 32 * STEP * a)).then_inc(s.shs, 1)
+    seen = [T.win[:, SEEN + 128 * STEP * t:SEEN + (128 * t + 32) * STEP:STEP] for t in (0, 1)]
+    for t in (0, 1):
+        v(V.memset(seen[t], NONE))
+    V.wait_ge(s.z0, 1)
     V.wait_ge(s.sx, 16)
-    V.quantize_mx(T.q[:, OWN:ALL], T.sq[:, OWN:ALL], T.xt[:]).then_inc(s.qx, 1)
+    V.quantize_mx(T.q[:, OWN - GAP:OWN + HEAD], T.sq[:, OWN - GAP:OWN + HEAD], T.xt[:, 0:512]).then_inc(s.qx, 1)
+    V.wait_ge(s.shs, 4)
+    V.wait_ge(s.sp, 32)
+    for a in (0, 64):
+        v(V.tensor_scalar(T.u[a:a + 64, :], T.own[0:64, :], float(STEP), T.sh[a:a + 64, :], A.mult, A.add))
+    V.wait_ge(s.sp2, 1)
+    vw()
+    v(V.tensor_tensor(T.off[:, 0:3], T.u[:], T.spare[:], A.max))
+    V.wait_ge(s.gi, 1)
     vw()
     v(V.tensor_copy(T.win[:].indirect(T.off[:, 0:3]), T.val[:]))
     vw()
-    v(V.transpose(T.tt[:], T.win[:, 192:256]))
-    vw()
-    V.tensor_tensor(T.land[:, me:me + 2], T.tt[:, 15:64:32], T.tt[:, 23:64:32], A.max).then_inc(s.ofs, 1)
-    V.memset(T.in2[0:32, :], 0.0).then_inc(s.ms0, 1)
-    V.memset(T.t2[0:32, :], 0.0).then_inc(s.ms0, 1)
-    V.memset(T.dl[:, 0:N - 1], float(-K)).then_inc(s.cs, 1)
-    V.wait_ge(s.gn, 1)
-    V.tensor_scalar(T.hm[0:32, 0:1], T.pf[0:32, 0:1], -48.0, None, A.is_lt).then_inc(s.hms, 1)
-    V.tensor_scalar(T.hm[0:32, 1:2], T.pf[0:32, 0:1], -48.0, None, A.is_ge).then_inc(s.hms, 1)
+    for t in (0, 1):
+        V.transpose(T.tt[:, t:64:2], seen[t]).then_inc(s.ofs, 1)
+    V.wait_ge(s.ofs, 2)
+    V.tensor_tensor(T.land[:, me:me + 2], T.tt[:, 30:32], T.tt[:, 46:48], A.max).then_inc(s.tab, 1)
+    V.wait_ge(s.z1, 1)
+    V.wait_ge(s.sx2, 16)
+    V.quantize_mx(T.q[:, OWN + HEAD:ALL], T.sq[:, OWN + HEAD:ALL], T.xt[:, 512:1024]).then_inc(s.qx2, 1)
     V.wait_ge(s.sb, 16)
     V.quantize_mx(T.q[:, 0:B], T.sq[:, 0:B], T.bt[:]).then_inc(s.qb, 1)
     for o in range(O):
@@ -139,48 +148,66 @@ def rank_program(g, core, T, topo):
         V.quantize_mx(T.wq[:, 128 * o:128 * o + 128], T.wsq[:, 128 * o:128 * o + 128],
                       T.wt[:, 512 * o:512 * o + 512]).then_inc(s["qw%d" % o], 1)
 
+    def fill(out, value):
+        return S.activation(out, T.xt[0:out.shape[0], 0:out.shape[1]], Copy, bias=value)
+
     S.wait_ge(s.shs, 4)
-    S.wait_ge(s.gn, 1)
-    S.activation(T.dl[:, N - 1:N], T.sh[:], Copy, bias=640.0, scale=0.5).then_inc(s.cs, 1)
-    for t in (0, 1):
-        S.activation(T.ini[:, t:t + 1], T.sh[:], Identity, bias=T.pf[:, t:t + 1], scale=-1.0).then_inc(s.cs, 1)
-    S.wait_ge(s.ms0, 2)
+    S.activation(T.sh2[:], T.sh[:], Copy, bias=-161.0, scale=65.0 / 64).then_inc(s.sp1, 1)
+    S.wait_ge(s.gd, 1)
+    S.wait_ge(s.sp1, 1)
+    S.activation(T.spare[:], T.nd[:], Identity, bias=T.sh2[:]).then_inc(s.sp2, 1)
+    S.wait_ge(s.z0, 1)
+    fill(T.xt[:, 4 * (GAP + K):1024], 0.0).then_inc(s.z1, 1)
+    fill(T.hm[:, 0:1], 0.0).then_inc(s.hms, 1)
+    fill(T.hm[:, 1:2], 1.0).then_inc(s.hms, 1)
+    fill(T.sc[:, 2 * N:], 0.0).then_inc(s.cs, 1)
+    fill(T.t2[:], 0.0).then_inc(s.cs, 1)
+    fill(T.dl[:, 0:N - 2], float(-K)).then_inc(s.cs, 1)
+    fill(T.dl[:, N - 2:N - 1], float(-K - GAP)).then_inc(s.cs, 1)
     S.wait_ge(s.hms, 2)
+    for a in range(4):
+        fill(T.hm[32 * a:32 * a + 16, 0:1], 1.0).then_inc(s.cs, 1)
+        fill(T.hm[32 * a:32 * a + 16, 1:2], 0.0).then_inc(s.cs, 1)
+    S.wait_ge(s.gn, 1)
+    S.activation(T.dl[:, N - 1:N], T.sh[:], Copy, bias=OWN - 97.0, scale=1.0 / STEP).then_inc(s.cs, 1)
+    for t in (0, 1):
+        S.activation(T.ini[:, t:t + 1], T.sh[:], Identity, bias=T.pf[:, t:t + 1], scale=-1.0 / STEP).then_inc(s.cs, 1)
+    S.wait_ge(s.cs, 15)
     S.wait_ge(s.qx, 1)
+    S.wait_ge(s.qx2, 1)
     S.wait_ge(s.qb, 1)
 
-    V.wait_ge(s.cs, 4)
-    V.wait_ge(s.ms0, 2)
-    V.wait_ge(s.ofs, 1)
+    V.wait_ge(s.cs, 15)
     V.wait_ge(s.qx, 1)
+    V.wait_ge(s.qx2, 1)
     V.wait_ge(s.qb, 1)
+    V.wait_ge(s.tab, 1)
     V.wait_ge(s.al, eng * (N - 1))
     for t in (0, 1):
-        V.tensor_tensor_scan(T.sc[:, N * t:N * t + N], T.land[:, t:8 * N:8], T.dl[:], T.ini[:, t:t + 1], A.max, A.add).then_inc(s.scn, 1)
+        V.tensor_tensor_scan(T.sc[:, t:2 * N:2], T.land[:, t:8 * N:8], T.dl[:], T.ini[:, t:t + 1], A.max, A.add).then_inc(s.scn, 1)
     V.wait_ge(s.scn, 2)
     S.wait_ge(s.scn, 2)
-    for a in range(4):
-        out, src = T.in2[0:32, 2 * a:2 * a + 2], T.sc[32 * a:32 * a + 32, N - 1:2 * N:N]
-        (V.tensor_copy(out, src) if a < 2 else S.activation(out, src, Copy)).then_inc(s.cp, 1)
-    V.wait_ge(s.cp, 4)
-    S.wait_ge(s.cp, 4)
-    v(V.transpose(T.t2[0:32, 16:48], T.in2[0:32, :]))
-    for h in (0, 1):
-        S.activation(T.mk[0:32, h:16:2], T.in2[0:32, 0:8], Identity, scale=T.hm[0:32, h:h + 1]).then_inc(s.mks, 1)
-    vw()
-    for h in (0, 1):
-        v(V.transpose(T.f2[0:32, h:64:2], T.t2[0:32, 32 * h:32 * h + 32]))
-    V.wait_ge(s.mks, 2)
+    end = 2 * N - 2
+    v(V.transpose(T.t2[:, 16:48], T.sc[:, end:end + 32]))
+    for i, (a, h) in enumerate((a, h) for a in range(4) for h in (0, 1)):
+        out, src, keep = T.mk[0:32, 2 * a + h:16:8], T.sc[32 * a:32 * a + 32, end:end + 2], T.hm[32 * a:32 * a + 32, h:h + 1]
+        (V.tensor_scalar(out, src, keep, None, A.mult) if i < 3 else S.activation(out, src, Identity, scale=keep)).then_inc(s.mks, 1)
     vw()
     for a in range(4):
-        V.tensor_tensor(T.pick[32 * a:32 * a + 32, :], T.f2[0:32, 0:16], T.mk[0:32, :], A.max).then_inc(s.offr, 1)
+        V.transpose(T.f2[0:32, 64 * a:64 * a + 64], T.t2[32 * a:32 * a + 32, :]).then_inc(s.tb, 1)
+    V.wait_ge(s.mks, 8)
+    V.wait_ge(s.tb, 4)
+    for t in (0, 1):
+        for a in range(4):
+            V.tensor_tensor(T.pick[32 * a:32 * a + 32, 8 * t:8 * t + 8], T.f2[0:32, t:256:32], T.mk[0:32, 8 * t:8 * t + 8],
+                            A.max).then_inc(s["offr%d" % t], 1)
 
     V.wait_ge(s.ac, eng * (N - 1))
-    V.wait_ge(s.offr, 4)
-    S.wait_ge(s.asc, eng * (N - 1))
-    S.wait_ge(s.offr, 4)
+    S.wait_ge(s.asc, eng * N)
     for h in (0, 1):
         o = T.pick[:, 8 * h:8 * h + 8]
+        V.wait_ge(s["offr%d" % h], 4)
+        S.wait_ge(s["offr%d" % h], 4)
         V.tensor_copy(T.m[:, 128 * h:128 * h + 128].bitcast(dt.uint32), T.q[:, 0:WIDE].bitcast(dt.uint32).indirect(o)).then_inc(s["pkv%d" % h], 1)
         S.activation(T.ms[:, 128 * h:128 * h + 128], T.sq[:, 0:WIDE].indirect(o), Copy).then_inc(s["pks%d" % h], 1)
 
@@ -203,4 +230,4 @@ def rank_program(g, core, T, topo):
         Y.dma_start(T.y[:, c:c + 128], T.ys[:, c:c + 128]).then_inc(s.sy, 16)
     Y.wait_ge(s.sy, 96)
     V.wait_ge(s.v, n[0])
-    g.wait_ge(s.loc, 4 * eng)
+    g.wait_ge(s.loc, 5 * eng)

@@ -1,19 +1,14 @@
 from concourse.bass import DstId, RemoteDMATransfer
-from concourse.mybir import dt, AluOpType, ActivationFunctionType
+from concourse.mybir import dt, AluOpType, AxisListType, ActivationFunctionType
 
 N, B, K, O = 6, 256, 96, 3
-HEAD = 16
+HEAD = 4
 GAP = 128 - HEAD
-OWN = B + K * (N - 1) + GAP
-WIDE = OWN + K
-ALL = OWN + HEAD + 128
-STEP = 64
-SEEN = 97 * STEP
-NONE = -1024.0
+ALL = B + 2 * K * N + GAP + HEAD + 128
 
 
-def slot(d):
-    return B + K * (N - 1 - d)
+def column(s, r):
+    return B + K * (s + 1) + (K * N if s <= r else 0) + (GAP if s == r else 0)
 
 
 SCRATCH = {
@@ -29,28 +24,21 @@ SCRATCH = {
     "ys": ("sbuf", [128, O * B], "float32"),
     "ps": ("psum", [128, 3072], "float32"),
     "own": ("sbuf", [128, 3], "int32"),
-    "nd": ("sbuf", [128, 3], "float32"),
-    "spare": ("sbuf", [128, 3], "float32"),
-    "sh": ("sbuf", [128, 1], "float32"),
-    "sh2": ("sbuf", [128, 1], "float32"),
-    "u": ("sbuf", [128, 3], "float32"),
-    "off": ("sbuf", [128, 4], "uint16"),
-    "val": ("sbuf", [128, 48], "bfloat16"),
-    "win": ("sbuf", [128, SEEN + STEP * B], "bfloat16"),
-    "tt": ("sbuf", [128, 64], "bfloat16"),
-    "land": ("sbuf", [128, 8 * N], "bfloat16"),
+    "row": ("sbuf", [128, 32], "int32"),
+    "num": ("sbuf", [128, 32], "int32"),
+    "at0": ("sbuf", [128, 64], "bfloat16"),
+    "at": ("sbuf", [128, 2, 32], "bfloat16"),
+    "hit": ("sbuf", [128, 2, 3, 32], "uint16"),
+    "tt": ("sbuf", [128, 2, 96], "uint16"),
+    "up": ("sbuf", [128, 4], "float32"),
+    "land": ("sbuf", [128, 16, 8], "uint16"),
     "pf": ("sbuf", [128, 2], "float32"),
-    "ini": ("sbuf", [128, 2], "float32"),
-    "dl": ("sbuf", [128, N], "float32"),
-    "hm": ("sbuf", [128, 2], "float32"),
-    "sc": ("sbuf", [128, 2 * N + 30], "float32"),
-    "t2": ("sbuf", [128, 64], "float32"),
-    "mk": ("sbuf", [128, 16], "float32"),
-    "f2": ("sbuf", [128, 256], "float32"),
+    "t2": ("sbuf", [128, 2, 2, 16], "uint16"),
+    "f2": ("sbuf", [128, 8, 32], "uint16"),
     "pick": ("sbuf", [128, 16], "uint16"),
 }
-SEMAPHORES = ["sx", "sx2", "sb", "sw", "sw2", "sp", "sp1", "sp2", "gd", "gi", "gn", "z0", "z1", "v", "qx", "qx2", "qb", "qw0", "qw1",
-              "qw2", "al", "ac", "asc", "loc", "ofs", "shs", "cs", "scn", "hms", "mks", "tb", "tab", "offr0", "offr1",
+SEMAPHORES = ["sx", "sx2", "sb", "sw", "sw2", "sp", "gd", "gi", "ats", "gn", "z0", "z1", "v", "qx", "qx2", "qb", "qw0", "qw1",
+              "qw2", "al", "ac", "asc", "loc", "fl", "tb", "tab", "tab1", "offr0", "offr1",
               "pkv0", "pkv1", "pks0", "pks1", "sy"]
 SEMAPHORES += ["mm%d" % i for i in range(6)] + ["c%d" % i for i in range(6)]
 
@@ -61,7 +49,12 @@ def rank_program(g, core, T, topo):
         return
     A, s = AluOpType, T.sem
     V, S, P, Y = g.vector, g.scalar, g.tensor, g.sync
-    Copy, Identity = ActivationFunctionType.Copy, ActivationFunctionType.Identity
+    Copy = ActivationFunctionType.Copy
+    mine, at_b = column(r, r), K * (r + 2)
+    wide = mine + K
+
+    def cell(i):
+        return T.land[:, i, 0:2]
 
     Y.dma_start(T.xt[:, 4 * GAP:512], T.x[:, 0:4 * HEAD]).then_inc(s.sx, 16)
     for a, e in ((0, S), (1, Y)):
@@ -81,125 +74,110 @@ def rank_program(g, core, T, topo):
         V.wait_ge(s.v, n[0])
 
     imprecise = {"allow_small_or_imprecise_dtypes": True}
-    g.iota(T.nd[:], [[16, 3]], 0, 1, **imprecise).then_inc(s.gd, 1)
-    g.iota(T.val[:], [[16, 3], [1, 8], [48, 2]], -15, 1, **imprecise).then_inc(s.gi, 1)
-    g.iota(T.pf[:], [[128, 2]], -159, 1, **imprecise).then_inc(s.gn, 1)
-
     others = [(r + 1 + i) % N for i in range(N - 1)]
-    ids, mask = [], None
+    many, few = sorted(([o for o in others if o < r], [o for o in others if o > r]), key=len, reverse=True)
+    first = column(r, many[0])
+    second = column(r, few[0]) if few else first
+    g.iota(T.at0[:], [[128, 2], [1, 32]], 0, 0, **imprecise).then_inc(s.gi, 1)
+    g.iota(T.row[:], [[1, 16], [48, 2]], first, 16).then_inc(s.gd, 1)
+    g.iota(T.pf[:], [[128, 2]], at_b, 1, **imprecise).then_inc(s.gn, 1)
+
+    ids, mask = {}, None
     for o in others:
         rid, pid, _se = topo.addr(T.cores[o])
-        ids.append(DstId(rid=rid, pnc=pid))
+        ids[o] = DstId(rid=rid, pnc=pid)
         k = topo.mask(core, T.cores[o])
         mask = k if mask is None else mask & k
     eng = len([e for e in topo.engines(core, T.cores[others[0]])])
-    ds = [(o - r) % N for o in others]
+    calls = [0]
 
-    def send(src, dst, sem, a=0, b=N - 1, other=None):
-        g.remote_dma_fused([RemoteDMATransfer(dst_ids=ids[a:b], dma_engine_mask=mask, remote_sem=sem,
-                                              srcs=[src] if other is None else [src, other], alu_op=0 if other is None else 2,
-                                              dsts=[dst(d) for d in ds[a:b]])], local_sem=s.loc)
+    def send(src, dst, sem, to):
+        calls[0] += 1
+        g.remote_dma_fused([RemoteDMATransfer(dst_ids=[ids[o] for o in to], dma_engine_mask=mask, remote_sem=sem, srcs=[src],
+                                              dsts=[dst(o) for o in to])], local_sem=s.loc)
 
-    def scales(d):
-        return T.sq[:, slot(d):slot(d) + K]
+    def scales(a, b, to):
+        send(T.sq[:, mine + a:mine + b], lambda o: T.sq[:, column(r, o) + a:column(r, o) + b], s.asc, to)
 
-    me = 8 * (N - 1)
     g.wait_ge(s.qx, 1)
-    send(T.sq[:, OWN:OWN + HEAD], lambda d: T.sq[:, slot(d):slot(d) + HEAD], s.asc, 0, 1)
-    g.wait_ge(s.tab, 1)
-    send(T.land[:, me:me + 2], lambda d: T.land[:, 8 * (N - 1 - d):8 * (N - 1 - d) + 2], s.al)
+    scales(0, HEAD, others[:1])
     g.wait_ge(s.qx2, 1)
-    send(T.q[:, OWN:WIDE].bitcast(dt.uint8), lambda d: T.q[:, slot(d):slot(d) + K].bitcast(dt.uint8), s.ac)
-    send(T.sq[:, OWN:WIDE], scales, s.asc, 1)
-    send(T.sq[:, OWN + HEAD:WIDE], lambda d: T.sq[:, slot(d) + HEAD:slot(d) + K], s.asc, 0, 1)
+    g.wait_ge(s.tab1, 1)
+    send(cell(3), lambda o: cell(4 + (o - r) % N), s.al, many)
+    if few:
+        g.wait_ge(s.tab, 1)
+        send(cell(1), lambda o: cell(4 + (o - r) % N), s.al, few)
+    send(T.q[:, mine:wide].bitcast(dt.uint8), lambda o: T.q[:, column(r, o):column(r, o) + K].bitcast(dt.uint8), s.ac, others)
+    scales(HEAD, K, others[:1])
+    scales(0, K, others[1:])
 
     V.memset(T.xt[:, 0:4 * GAP], 0.0).then_inc(s.z0, 1)
-    for a in range(4):
-        V.memset(T.sh[32 * a:32 * a + 32, :], float(SEEN - 32 * STEP * a)).then_inc(s.shs, 1)
-    seen = [T.win[:, SEEN + 128 * STEP * t:SEEN + (128 * t + 32) * STEP:STEP] for t in (0, 1)]
-    for t in (0, 1):
-        v(V.memset(seen[t], NONE))
+    V.wait_ge(s.gd, 1)
+    for a in (0, 32):
+        v(V.transpose(T.num[a:a + 32, :], T.row[0:32, :]))
+    vw()
     V.wait_ge(s.z0, 1)
     V.wait_ge(s.sx, 16)
-    V.quantize_mx(T.q[:, OWN - GAP:OWN + HEAD], T.sq[:, OWN - GAP:OWN + HEAD], T.xt[:, 0:512]).then_inc(s.qx, 1)
-    V.wait_ge(s.shs, 4)
+    V.quantize_mx(T.q[:, mine - GAP:mine + HEAD], T.sq[:, mine - GAP:mine + HEAD], T.xt[:, 0:512]).then_inc(s.qx, 1)
+    V.wait_ge(s.ats, 4)
     V.wait_ge(s.sp, 32)
     for a in (0, 64):
-        v(V.tensor_scalar(T.u[a:a + 64, :], T.own[0:64, :], float(STEP), T.sh[a:a + 64, :], A.mult, A.add))
-    V.wait_ge(s.sp2, 1)
-    vw()
-    v(V.tensor_tensor(T.off[:, 0:3], T.u[:], T.spare[:], A.max))
-    V.wait_ge(s.gi, 1)
-    vw()
-    v(V.tensor_copy(T.win[:].indirect(T.off[:, 0:3]), T.val[:]))
-    vw()
-    for t in (0, 1):
-        V.transpose(T.tt[:, t:64:2], seen[t]).then_inc(s.ofs, 1)
-    V.wait_ge(s.ofs, 2)
-    V.tensor_tensor(T.land[:, me:me + 2], T.tt[:, 30:32], T.tt[:, 46:48], A.max).then_inc(s.tab, 1)
+        for c in range(3):
+            v(V.tensor_scalar(T.hit[a:a + 64, :, c, :], T.at[a:a + 64, :, :], T.own[0:64, c:c + 1], T.num[0:64, c:c + 1], A.is_equal, A.mult))
     V.wait_ge(s.z1, 1)
     V.wait_ge(s.sx2, 16)
-    V.quantize_mx(T.q[:, OWN + HEAD:ALL], T.sq[:, OWN + HEAD:ALL], T.xt[:, 512:1024]).then_inc(s.qx2, 1)
+    V.quantize_mx(T.q[:, mine + HEAD:mine + HEAD + 128], T.sq[:, mine + HEAD:mine + HEAD + 128], T.xt[:, 512:1024]).then_inc(s.qx2, 1)
+    vw()
+    v(V.transpose(T.tt[:], T.hit[:]))
+    vw()
+    V.tensor_reduce(cell(3), T.tt[:], AxisListType.X, A.max).then_inc(s.tab1, 1)
+    V.wait_ge(s.tab1, 1)
+    V.tensor_scalar(cell(1), cell(3), float(second - first), None, A.add).then_inc(s.tab, 1)
+    v(V.tensor_scalar(T.up[:, 0:2], cell(3), 0.0, float(mine - first), A.is_gt, A.mult))
     V.wait_ge(s.sb, 16)
-    V.quantize_mx(T.q[:, 0:B], T.sq[:, 0:B], T.bt[:]).then_inc(s.qb, 1)
+    V.quantize_mx(T.q[:, at_b:at_b + B], T.sq[:, at_b:at_b + B], T.bt[:]).then_inc(s.qb, 1)
+    vw()
+    v(V.tensor_tensor(T.up[:, 2:4], T.up[:, 0:2], cell(3), A.add))
     for o in range(O):
         if o < 2:
             V.wait_ge(s.sw2 if o else s.sw, 16)
         V.quantize_mx(T.wq[:, 128 * o:128 * o + 128], T.wsq[:, 128 * o:128 * o + 128],
                       T.wt[:, 512 * o:512 * o + 512]).then_inc(s["qw%d" % o], 1)
+        if o == 0:
+            V.wait_ge(s.gn, 1)
+            vw()
+            v(V.tensor_tensor(cell(4), T.up[:, 2:4], T.pf[:], A.max))
 
     def fill(out, value):
         return S.activation(out, T.xt[0:out.shape[0], 0:out.shape[1]], Copy, bias=value)
 
-    S.wait_ge(s.shs, 4)
-    S.activation(T.sh2[:], T.sh[:], Copy, bias=-161.0, scale=65.0 / 64).then_inc(s.sp1, 1)
-    S.wait_ge(s.gd, 1)
-    S.wait_ge(s.sp1, 1)
-    S.activation(T.spare[:], T.nd[:], Identity, bias=T.sh2[:]).then_inc(s.sp2, 1)
+    S.wait_ge(s.gi, 1)
+    for a in range(0, 128, 32):
+        S.activation(T.at[a:a + 32, :, :], T.at0[a:a + 32, :], Copy, bias=float(a)).then_inc(s.ats, 1)
     S.wait_ge(s.z0, 1)
     fill(T.xt[:, 4 * (GAP + K):1024], 0.0).then_inc(s.z1, 1)
-    fill(T.hm[:, 0:1], 0.0).then_inc(s.hms, 1)
-    fill(T.hm[:, 1:2], 1.0).then_inc(s.hms, 1)
-    fill(T.sc[:, 2 * N:], 0.0).then_inc(s.cs, 1)
-    fill(T.t2[:], 0.0).then_inc(s.cs, 1)
-    fill(T.dl[:, 0:N - 2], float(-K)).then_inc(s.cs, 1)
-    fill(T.dl[:, N - 2:N - 1], float(-K - GAP)).then_inc(s.cs, 1)
-    S.wait_ge(s.hms, 2)
-    for a in range(4):
-        fill(T.hm[32 * a:32 * a + 16, 0:1], 1.0).then_inc(s.cs, 1)
-        fill(T.hm[32 * a:32 * a + 16, 1:2], 0.0).then_inc(s.cs, 1)
-    S.wait_ge(s.gn, 1)
-    S.activation(T.dl[:, N - 1:N], T.sh[:], Copy, bias=OWN - 97.0, scale=1.0 / STEP).then_inc(s.cs, 1)
-    for t in (0, 1):
-        S.activation(T.ini[:, t:t + 1], T.sh[:], Identity, bias=T.pf[:, t:t + 1], scale=-1.0 / STEP).then_inc(s.cs, 1)
-    S.wait_ge(s.cs, 15)
+    for i in (0, 2, 10, 11, 12, 13, 14, 15):
+        fill(cell(i), 0.0).then_inc(s.fl, 1)
     S.wait_ge(s.qx, 1)
     S.wait_ge(s.qx2, 1)
     S.wait_ge(s.qb, 1)
 
-    V.wait_ge(s.cs, 15)
+    V.wait_ge(s.fl, 8)
+    V.wait_ge(s.tab, 1)
     V.wait_ge(s.qx, 1)
     V.wait_ge(s.qx2, 1)
     V.wait_ge(s.qb, 1)
-    V.wait_ge(s.tab, 1)
+    vw()
     V.wait_ge(s.al, eng * (N - 1))
-    for t in (0, 1):
-        V.tensor_tensor_scan(T.sc[:, t:2 * N:2], T.land[:, t:8 * N:8], T.dl[:], T.ini[:, t:t + 1], A.max, A.add).then_inc(s.scn, 1)
-    V.wait_ge(s.scn, 2)
-    S.wait_ge(s.scn, 2)
-    end = 2 * N - 2
-    v(V.transpose(T.t2[:, 16:48], T.sc[:, end:end + 32]))
-    for i, (a, h) in enumerate((a, h) for a in range(4) for h in (0, 1)):
-        out, src, keep = T.mk[0:32, 2 * a + h:16:8], T.sc[32 * a:32 * a + 32, end:end + 2], T.hm[32 * a:32 * a + 32, h:h + 1]
-        (V.tensor_scalar(out, src, keep, None, A.mult) if i < 3 else S.activation(out, src, Identity, scale=keep)).then_inc(s.mks, 1)
+    for c in (0, 1):
+        v(V.transpose(T.t2[:, :, c, :], T.land[:, :, 0:2]))
     vw()
     for a in range(4):
-        V.transpose(T.f2[0:32, 64 * a:64 * a + 64], T.t2[32 * a:32 * a + 32, :]).then_inc(s.tb, 1)
-    V.wait_ge(s.mks, 8)
+        V.transpose(T.f2[0:32, 2 * a:2 * a + 2, :], T.t2[32 * a:32 * a + 32, :, :, :]).then_inc(s.tb, 1)
     V.wait_ge(s.tb, 4)
     for t in (0, 1):
         for a in range(4):
-            V.tensor_tensor(T.pick[32 * a:32 * a + 32, 8 * t:8 * t + 8], T.f2[0:32, t:256:32], T.mk[0:32, 8 * t:8 * t + 8],
+            V.tensor_reduce(T.pick[32 * a:32 * a + 32, 8 * t:8 * t + 8], T.f2[0:32, :, 8 + t:20:2], AxisListType.X,
                             A.max).then_inc(s["offr%d" % t], 1)
 
     V.wait_ge(s.ac, eng * (N - 1))
@@ -208,10 +186,11 @@ def rank_program(g, core, T, topo):
         o = T.pick[:, 8 * h:8 * h + 8]
         V.wait_ge(s["offr%d" % h], 4)
         S.wait_ge(s["offr%d" % h], 4)
-        V.tensor_copy(T.m[:, 128 * h:128 * h + 128].bitcast(dt.uint32), T.q[:, 0:WIDE].bitcast(dt.uint32).indirect(o)).then_inc(s["pkv%d" % h], 1)
-        S.activation(T.ms[:, 128 * h:128 * h + 128], T.sq[:, 0:WIDE].indirect(o), Copy).then_inc(s["pks%d" % h], 1)
+        V.tensor_copy(T.m[:, 128 * h:128 * h + 128].bitcast(dt.uint32), T.q[:, 0:wide].bitcast(dt.uint32).indirect(o)).then_inc(s["pkv%d" % h], 1)
+        S.activation(T.ms[:, 128 * h:128 * h + 128], T.sq[:, 0:wide].indirect(o), Copy).then_inc(s["pks%d" % h], 1)
 
     seq = [(h, o) for h in (0, 1) for o in range(O)]
+    stores = {0: (0, 1), 1: (2, 3), 3: (1, 2), 5: (3, 6)}
     for o in range(O):
         P.wait_ge(s["qw%d" % o], 1)
     for i, (h, o) in enumerate(seq):
@@ -221,13 +200,15 @@ def rank_program(g, core, T, topo):
         P.matmul_mx(T.ps[:, 512 * i:512 * i + 128], T.wq[:, 128 * o:128 * o + 128], T.wsq[:, 128 * o:128 * o + 128],
                     T.m[:, 128 * h:128 * h + 128], T.ms[:, 128 * h:128 * h + 128], True, True).then_inc(s["mm%d" % i], 1)
     for i, (h, o) in enumerate(seq):
-        e = V if i in (0, 2, 4) else S
+        e = S if i in (2, 4) else V
         c = 256 * o + 128 * h
         e.wait_ge(s["mm%d" % i], 1)
         out, src = T.ys[:, c:c + 128], T.ps[:, 512 * i:512 * i + 128]
         (V.tensor_copy(out, src) if e is V else S.activation(out, src, Copy)).then_inc(s["c%d" % i], 1)
         Y.wait_ge(s["c%d" % i], 1)
-        Y.dma_start(T.y[:, c:c + 128], T.ys[:, c:c + 128]).then_inc(s.sy, 16)
-    Y.wait_ge(s.sy, 96)
+        if i in stores:
+            a, b = stores[i]
+            Y.dma_start(T.y[:, 128 * a:128 * b], T.ys[:, 128 * a:128 * b]).then_inc(s.sy, 16)
+    Y.wait_ge(s.sy, 16 * len(stores))
     V.wait_ge(s.v, n[0])
-    g.wait_ge(s.loc, 5 * eng)
+    g.wait_ge(s.loc, calls[0] * eng)

from concourse.bass import DstId, RemoteDMATransfer
from concourse.mybir import dt, AluOpType, AxisListType, ActivationFunctionType

N, B, K, O = 6, 256, 96, 3
HEAD = 4
GAP = 128 - HEAD
ALL = B + 2 * K * N + GAP + HEAD + 128


def column(s, r):
    return B + K * (s + 1) + (K * N if s <= r else 0) + (GAP if s == r else 0)


SCRATCH = {
    "xt": ("sbuf", [128, 1024], "bfloat16"),
    "bt": ("sbuf", [128, 4 * B], "bfloat16"),
    "wt": ("sbuf", [128, 512 * O], "bfloat16"),
    "q": ("sbuf", [128, ALL], "float8_e4m3fn_x4"),
    "sq": ("sbuf", [128, ALL], "uint8"),
    "wq": ("sbuf", [128, 128 * O], "float8_e4m3fn_x4"),
    "wsq": ("sbuf", [128, 128 * O], "uint8"),
    "m": ("sbuf", [128, B], "float8_e4m3fn_x4"),
    "ms": ("sbuf", [128, B], "uint8"),
    "ys": ("sbuf", [128, O * B], "float32"),
    "ps": ("psum", [128, 3072], "float32"),
    "own": ("sbuf", [128, 3], "int32"),
    "row": ("sbuf", [128, 32], "int32"),
    "num": ("sbuf", [128, 32], "int32"),
    "at0": ("sbuf", [128, 64], "bfloat16"),
    "at": ("sbuf", [128, 2, 32], "bfloat16"),
    "hit": ("sbuf", [128, 2, 3, 32], "uint16"),
    "tt": ("sbuf", [128, 2, 96], "uint16"),
    "up": ("sbuf", [128, 4], "float32"),
    "land": ("sbuf", [128, 16, 8], "uint16"),
    "pf": ("sbuf", [128, 2], "float32"),
    "t2": ("sbuf", [128, 2, 2, 16], "uint16"),
    "f2": ("sbuf", [128, 8, 32], "uint16"),
    "pick": ("sbuf", [128, 16], "uint16"),
}
SEMAPHORES = ["sx", "sx2", "sb", "sw", "sw2", "sp", "gd", "gi", "ats", "gn", "z0", "z1", "v", "qx", "qx2", "qb", "qw0", "qw1",
              "qw2", "al", "ac", "asc", "loc", "fl", "tb", "tab", "tab1", "offr0", "offr1",
              "pkv0", "pkv1", "pks0", "pks1", "sy"]
SEMAPHORES += ["mm%d" % i for i in range(6)] + ["c%d" % i for i in range(6)]


def rank_program(g, core, T, topo):
    r = T.rank_of(core)
    if r is None:
        return
    A, s = AluOpType, T.sem
    V, S, P, Y = g.vector, g.scalar, g.tensor, g.sync
    Copy = ActivationFunctionType.Copy
    mine, at_b = column(r, r), K * (r + 2)
    wide = mine + K

    def cell(i):
        return T.land[:, i, 0:2]

    Y.dma_start(T.xt[:, 4 * GAP:512], T.x[:, 0:4 * HEAD]).then_inc(s.sx, 16)
    for a, e in ((0, S), (1, Y)):
        e.dma_start(T.own[32 * a:32 * a + 32, :], T.pl[:]).then_inc(s.sp, 16)
    Y.dma_start(T.xt[:, 512:4 * (GAP + K)], T.x[:, 4 * HEAD:4 * K]).then_inc(s.sx2, 16)
    Y.dma_start(T.bt[:], T.b[:]).then_inc(s.sb, 16)
    Y.dma_start(T.wt[:, 0:512], T.w[:, 0:512]).then_inc(s.sw, 16)
    Y.dma_start(T.wt[:, 512:1536], T.w[:, 512:1536]).then_inc(s.sw2, 16)

    n = [0]

    def v(ins):
        n[0] += 1
        return ins.then_inc(s.v, 1)

    def vw():
        V.wait_ge(s.v, n[0])

    imprecise = {"allow_small_or_imprecise_dtypes": True}
    others = [(r + 1 + i) % N for i in range(N - 1)]
    many, few = sorted(([o for o in others if o < r], [o for o in others if o > r]), key=len, reverse=True)
    first = column(r, many[0])
    second = column(r, few[0]) if few else first
    g.iota(T.at0[:], [[128, 2], [1, 32]], 0, 0, **imprecise).then_inc(s.gi, 1)
    g.iota(T.row[:], [[1, 16], [48, 2]], first, 16).then_inc(s.gd, 1)
    g.iota(T.pf[:], [[128, 2]], at_b, 1, **imprecise).then_inc(s.gn, 1)

    ids, mask = {}, None
    for o in others:
        rid, pid, _se = topo.addr(T.cores[o])
        ids[o] = DstId(rid=rid, pnc=pid)
        k = topo.mask(core, T.cores[o])
        mask = k if mask is None else mask & k
    eng = len([e for e in topo.engines(core, T.cores[others[0]])])
    calls = [0]

    def send(src, dst, sem, to):
        calls[0] += 1
        g.remote_dma_fused([RemoteDMATransfer(dst_ids=[ids[o] for o in to], dma_engine_mask=mask, remote_sem=sem, srcs=[src],
                                              dsts=[dst(o) for o in to])], local_sem=s.loc)

    def scales(a, b, to):
        send(T.sq[:, mine + a:mine + b], lambda o: T.sq[:, column(r, o) + a:column(r, o) + b], s.asc, to)

    g.wait_ge(s.qx, 1)
    scales(0, HEAD, others[:1])
    g.wait_ge(s.qx2, 1)
    g.wait_ge(s.tab1, 1)
    send(cell(3), lambda o: cell(4 + (o - r) % N), s.al, many)
    if few:
        g.wait_ge(s.tab, 1)
        send(cell(1), lambda o: cell(4 + (o - r) % N), s.al, few)
    send(T.q[:, mine:wide].bitcast(dt.uint8), lambda o: T.q[:, column(r, o):column(r, o) + K].bitcast(dt.uint8), s.ac, others)
    scales(HEAD, K, others[:1])
    scales(0, K, others[1:])

    V.memset(T.xt[:, 0:4 * GAP], 0.0).then_inc(s.z0, 1)
    V.wait_ge(s.gd, 1)
    for a in (0, 32):
        v(V.transpose(T.num[a:a + 32, :], T.row[0:32, :]))
    vw()
    V.wait_ge(s.z0, 1)
    V.wait_ge(s.sx, 16)
    V.quantize_mx(T.q[:, mine - GAP:mine + HEAD], T.sq[:, mine - GAP:mine + HEAD], T.xt[:, 0:512]).then_inc(s.qx, 1)
    V.wait_ge(s.ats, 4)
    V.wait_ge(s.sp, 32)
    for a in (0, 64):
        for c in range(3):
            v(V.tensor_scalar(T.hit[a:a + 64, :, c, :], T.at[a:a + 64, :, :], T.own[0:64, c:c + 1], T.num[0:64, c:c + 1], A.is_equal, A.mult))
    V.wait_ge(s.z1, 1)
    V.wait_ge(s.sx2, 16)
    V.quantize_mx(T.q[:, mine + HEAD:mine + HEAD + 128], T.sq[:, mine + HEAD:mine + HEAD + 128], T.xt[:, 512:1024]).then_inc(s.qx2, 1)
    vw()
    v(V.transpose(T.tt[:], T.hit[:]))
    vw()
    V.tensor_reduce(cell(3), T.tt[:], AxisListType.X, A.max).then_inc(s.tab1, 1)
    V.wait_ge(s.tab1, 1)
    V.tensor_scalar(cell(1), cell(3), float(second - first), None, A.add).then_inc(s.tab, 1)
    v(V.tensor_scalar(T.up[:, 0:2], cell(3), 0.0, float(mine - first), A.is_gt, A.mult))
    V.wait_ge(s.sb, 16)
    V.quantize_mx(T.q[:, at_b:at_b + B], T.sq[:, at_b:at_b + B], T.bt[:]).then_inc(s.qb, 1)
    vw()
    v(V.tensor_tensor(T.up[:, 2:4], T.up[:, 0:2], cell(3), A.add))
    for o in range(O):
        if o < 2:
            V.wait_ge(s.sw2 if o else s.sw, 16)
        V.quantize_mx(T.wq[:, 128 * o:128 * o + 128], T.wsq[:, 128 * o:128 * o + 128],
                      T.wt[:, 512 * o:512 * o + 512]).then_inc(s["qw%d" % o], 1)
        if o == 0:
            V.wait_ge(s.gn, 1)
            vw()
            v(V.tensor_tensor(cell(4), T.up[:, 2:4], T.pf[:], A.max))

    def fill(out, value):
        return S.activation(out, T.xt[0:out.shape[0], 0:out.shape[1]], Copy, bias=value)

    S.wait_ge(s.gi, 1)
    for a in range(0, 128, 32):
        S.activation(T.at[a:a + 32, :, :], T.at0[a:a + 32, :], Copy, bias=float(a)).then_inc(s.ats, 1)
    S.wait_ge(s.z0, 1)
    fill(T.xt[:, 4 * (GAP + K):1024], 0.0).then_inc(s.z1, 1)
    for i in (0, 2, 10, 11, 12, 13, 14, 15):
        fill(cell(i), 0.0).then_inc(s.fl, 1)
    S.wait_ge(s.qx, 1)
    S.wait_ge(s.qx2, 1)
    S.wait_ge(s.qb, 1)

    V.wait_ge(s.fl, 8)
    V.wait_ge(s.tab, 1)
    V.wait_ge(s.qx, 1)
    V.wait_ge(s.qx2, 1)
    V.wait_ge(s.qb, 1)
    vw()
    V.wait_ge(s.al, eng * (N - 1))
    for c in (0, 1):
        v(V.transpose(T.t2[:, :, c, :], T.land[:, :, 0:2]))
    vw()
    for a in range(4):
        V.transpose(T.f2[0:32, 2 * a:2 * a + 2, :], T.t2[32 * a:32 * a + 32, :, :, :]).then_inc(s.tb, 1)
    V.wait_ge(s.tb, 4)
    for t in (0, 1):
        for a in range(4):
            V.tensor_reduce(T.pick[32 * a:32 * a + 32, 8 * t:8 * t + 8], T.f2[0:32, :, 8 + t:20:2], AxisListType.X,
                            A.max).then_inc(s["offr%d" % t], 1)

    V.wait_ge(s.ac, eng * (N - 1))
    S.wait_ge(s.asc, eng * N)
    for h in (0, 1):
        o = T.pick[:, 8 * h:8 * h + 8]
        V.wait_ge(s["offr%d" % h], 4)
        S.wait_ge(s["offr%d" % h], 4)
        V.tensor_copy(T.m[:, 128 * h:128 * h + 128].bitcast(dt.uint32), T.q[:, 0:wide].bitcast(dt.uint32).indirect(o)).then_inc(s["pkv%d" % h], 1)
        S.activation(T.ms[:, 128 * h:128 * h + 128], T.sq[:, 0:wide].indirect(o), Copy).then_inc(s["pks%d" % h], 1)

    seq = [(h, o) for h in (0, 1) for o in range(O)]
    stores = {0: (0, 1), 1: (2, 3), 3: (1, 2), 5: (3, 6)}
    for o in range(O):
        P.wait_ge(s["qw%d" % o], 1)
    for i, (h, o) in enumerate(seq):
        if o == 0:
            P.wait_ge(s["pkv%d" % h], 1)
            P.wait_ge(s["pks%d" % h], 1)
        P.matmul_mx(T.ps[:, 512 * i:512 * i + 128], T.wq[:, 128 * o:128 * o + 128], T.wsq[:, 128 * o:128 * o + 128],
                    T.m[:, 128 * h:128 * h + 128], T.ms[:, 128 * h:128 * h + 128], True, True).then_inc(s["mm%d" % i], 1)
    for i, (h, o) in enumerate(seq):
        e = S if i in (2, 4) else V
        c = 256 * o + 128 * h
        e.wait_ge(s["mm%d" % i], 1)
        out, src = T.ys[:, c:c + 128], T.ps[:, 512 * i:512 * i + 128]
        (V.tensor_copy(out, src) if e is V else S.activation(out, src, Copy)).then_inc(s["c%d" % i], 1)
        Y.wait_ge(s["c%d" % i], 1)
        if i in stores:
            a, b = stores[i]
            Y.dma_start(T.y[:, 128 * a:128 * b], T.ys[:, 128 * a:128 * b]).then_inc(s.sy, 16)
    Y.wait_ge(s.sy, 16 * len(stores))
    V.wait_ge(s.v, n[0])
    g.wait_ge(s.loc, calls[0] * eng)
